import numpy as np
import ml_dtypes


def mxq(x, axis, fmt="e4m3"):
    dtype, down = {"e4m3": (ml_dtypes.float8_e4m3fn, 7), "e5m2": (ml_dtypes.float8_e5m2, 14)}[fmt]
    v = np.moveaxis(np.asarray(x, np.float32).astype(ml_dtypes.bfloat16).astype(np.float64), axis, -1)
    blocks = v.reshape(v.shape[:-1] + (-1, 32))
    amax = np.abs(blocks).max(-1, keepdims=True)
    byte = np.maximum(np.where(amax > 0, np.frexp(amax)[1] - 1 + 127, 0) - down, 1)
    scale = np.exp2(byte - 127.0)
    codes = (blocks / scale).astype(np.float32).astype(dtype).astype(np.float64)
    return np.moveaxis((codes * scale).reshape(v.shape), -1, axis)


WIDE = False


def mx_kscale(k):
    if not WIDE:
        return np.ones(k)
    levels = np.array([10, -10, 5, -5, 0])
    if k % 512:
        return np.exp2(np.random.permutation(np.resize(levels, k // 32))).repeat(32)
    a = np.empty((k // 512, 16))
    for p in range(k // 512):
        a[p, :8] = np.random.permutation(np.resize(levels, 8))
        for g in range(8):
            far = levels[np.abs(levels - a[p, g]) >= 10]
            a[p, g + 8] = far[np.random.randint(len(far))]
    return np.exp2(a.ravel()).repeat(32)


def f64(x):
    return np.asarray(x).astype(np.float64)


def striped(idx):
    return np.tile(np.asarray(idx).reshape(-1, 16).T, (8, 1)).astype(np.uint16)


def unstriped(offs):
    return offs[:16].T.reshape(-1).astype(np.int64)


B, N, T, D, DV, NQ = 1, 512, 2048, 256, 512, 512


def setup_inputs():
    n = np.random.standard_normal
    idx = np.random.permutation(T)[:B * N]
    s = mx_kscale(DV)[:, None]
    z = mx_kscale(NQ)[:, None]
    p = np.exp(n((B, NQ, N)))
    p = p / p.mean(2, keepdims=True)
    return {
        "doT": (n((B, DV, NQ)) * s / np.sqrt(DV)).astype(np.float32),
        "vT": (n((DV, T)) / s).astype(np.float32),
        "p": (p * z / np.sqrt(NQ)).astype(np.float32),
        "delta": (0.3 * n((B, NQ, 1))).astype(np.float32),
        "qm": (n((B, NQ, D)) / z).astype(np.float32),
        "offs": striped(idx),
    }


def reference(doT, vT, p, delta, qm, offs):
    idx = unstriped(offs)
    pick = lambda x: x[:, idx].reshape(x.shape[0], B, N).transpose(1, 0, 2)
    dp = mxq(f64(doT), 1, "e4m3").transpose(0, 2, 1) @ mxq(pick(f64(vT)), 1, "e4m3")
    ds = f64(p) * (dp - f64(delta))
    dk = mxq(f64(qm), 1, "e4m3").transpose(0, 2, 1) @ mxq(ds, 1, "e4m3")
    out = np.zeros((D, T))
    out[:, idx] = dk.transpose(1, 0, 2).reshape(D, B * N)
    return out

@@ -1,0 +1,162 @@
+from contextlib import ExitStack
+
+import concourse.mybir as mybir
+
+NQ, N, T, D, DV = 512, 512, 2048, 256, 512
+FLOPS = 2 * NQ * N * DV + 2 * D * N * NQ
+
+F32 = mybir.dt.float32
+BF16 = mybir.dt.bfloat16
+U32 = mybir.dt.uint32
+U16 = mybir.dt.uint16
+U8 = mybir.dt.uint8
+FP8X4 = mybir.dt.float8_e4m3fn_x4
+MULT = mybir.AluOpType.mult
+SUB = mybir.AluOpType.subtract
+
+P = 128
+J = 4
+HALF = N // 2
+M_VECTOR = 88
+B_VECTOR = 144
+
+
+def tile_attend_bwd_kernel(tc, doT, vT, p, delta, qm, offs, out):
+    nc = tc.nc
+    with ExitStack() as ctx:
+        keep = ctx.enter_context(tc.tile_pool(name="keep", bufs=1))
+        psum = ctx.enter_context(tc.psum_pool(name="psum", bufs=1))
+
+        offsets = keep.tile([P, N // 16], U16, name="offsets")
+        v_view = vT.rearrange("(p t) n -> p t n", t=J)
+        v_planes = []
+        for t in range(J):
+            plane = keep.tile([P, T], F32, name=f"plane{t}")
+            nc.sync.dma_start(plane[:], v_view[:, t, :])
+            v_planes.append(plane)
+            if t == 0:
+                nc.sync.dma_start(offsets[:], offs)
+        do_raw = keep.tile([P, J, NQ], F32, name="do_raw")
+        nc.sync.dma_start(do_raw[:], doT[0].rearrange("(p j) q -> p j q", j=J))
+        delta_sb = keep.tile([P, J], F32, name="delta_sb")
+        nc.sync.dma_start(delta_sb[:], delta[0].rearrange("(p t) o -> p (t o)", t=J))
+        p_view = p[0].rearrange("(p t) n -> p t n", t=J)
+        p_halves = []
+        for h in range(2):
+            p_half = keep.tile([P, J, HALF], F32, name=f"p_half{h}")
+            nc.sync.dma_start(p_half[:], p_view[:, :, h * HALF : (h + 1) * HALF])
+            p_halves.append(p_half)
+            if h == 0:
+                q_raw = keep.tile([P, J, D], F32, name="q_raw")
+                nc.sync.dma_start(q_raw[:], qm[0].rearrange("(p t) d -> p t d", t=J))
+
+        windows = []
+        for b in range(2):
+            window = keep.tile([P, T], F32, name=f"window{b}")
+            (nc.vector if b == 0 else nc.gpsimd).memset(window[:], 0.0)
+            windows.append(window)
+
+        v_grouped = keep.tile([P, N, J], BF16, name="v_grouped", align_bytes=64)
+        for t in range(J - 1):
+            nc.vector.tensor_copy(v_grouped[:, :, t], v_planes[t][:].indirect(offsets[:]))
+        for h in range(2):
+            nc.vector.tensor_copy(
+                v_grouped[:, h * HALF : (h + 1) * HALF, J - 1],
+                v_planes[J - 1][:].indirect(offsets[:, h * 16 : (h + 1) * 16]),
+            )
+        v_codes = keep.tile([P, N], U32, name="v_codes", align_bytes=64)
+        v_scales = keep.tile([P, N], U8, name="v_scales", align_bytes=64)
+        for h in range(2):
+            cols = slice(h * HALF, (h + 1) * HALF)
+            nc.vector.quantize_mx(
+                out=v_codes[:, cols].bitcast(FP8X4),
+                scales=v_scales[:, cols],
+                in_=v_grouped[:, cols, :].rearrange("p n t -> p (n t)"),
+            )
+
+        do_grouped = keep.tile([P, J, P, J], BF16, name="do_grouped", align_bytes=64)
+        do_dst = do_grouped[:].rearrange("p t m j -> p m j t")
+        do_src = do_raw[:].rearrange("p j (m t) -> p m j t", t=J)
+        nc.vector.tensor_copy(do_dst[:, :M_VECTOR], do_src[:, :M_VECTOR])
+        nc.scalar.copy(do_dst[:, M_VECTOR:], do_src[:, M_VECTOR:])
+        do_flat = do_grouped[:].rearrange("p t m j -> p (t m j)")
+        do_codes = keep.tile([P, NQ], U32, name="do_codes", align_bytes=64)
+        do_scales = keep.tile([P, NQ], U8, name="do_scales", align_bytes=64)
+        for h in range(2):
+            w = slice(h * 256, (h + 1) * 256)
+            nc.vector.quantize_mx(
+                out=do_codes[:, w].bitcast(FP8X4), scales=do_scales[:, w], in_=do_flat[:, h * 1024 : (h + 1) * 1024]
+            )
+
+        q_grouped = keep.tile([P, D, J], BF16, name="q_grouped", align_bytes=64)
+        nc.scalar.copy(
+            q_grouped[:].rearrange("p (c i) t -> p c t i", i=4), q_raw[:].rearrange("p t (c i) -> p c t i", i=4)
+        )
+        q_codes = keep.tile([P, D], U32, name="q_codes", align_bytes=64)
+        q_scales = keep.tile([P, D], U8, name="q_scales", align_bytes=64)
+
+        nc.vector.quantize_mx(
+            out=q_codes[:].bitcast(FP8X4), scales=q_scales[:], in_=q_grouped[:].rearrange("p d t -> p (d t)")
+        )
+
+        part = [keep.tile([P, J, HALF], F32, name=f"part{h}") for h in range(2)]
+        ds_grouped = [keep.tile([P, HALF, J], BF16, name=f"ds_grouped{h}", align_bytes=64) for h in range(2)]
+        ds_codes = [keep.tile([P, HALF], U32, name=f"ds_codes{h}", align_bytes=64) for h in range(2)]
+        ds_scales = [keep.tile([P, HALF], U8, name=f"ds_scales{h}", align_bytes=64) for h in range(2)]
+        for h in range(2):
+            cols = slice(h * HALF, (h + 1) * HALF)
+            for t in range(J):
+                dp = psum.tile([P, HALF], F32, name=f"bank{4 * h + t}")
+                q_cols = slice(t * P, (t + 1) * P)
+                nc.tensor.matmul_mx(
+                    out=dp[:],
+                    lhsT=do_codes[:, q_cols].bitcast(FP8X4),
+                    lhsT_scale=do_scales[:, q_cols],
+                    rhs=v_codes[:, cols].bitcast(FP8X4),
+                    rhs_scale=v_scales[:, cols],
+                    start=True,
+                    stop=True,
+                )
+                nc.vector.scalar_tensor_tensor(
+                    part[h][:, t, :], dp[:], delta_sb[:, t : t + 1], p_halves[h][:, t, :], SUB, MULT
+                )
+
+        def group(copy, h, first, last):
+            copy(
+                ds_grouped[h][:, first:last].rearrange("p (c i) t -> p c t i", i=4),
+                part[h][:, :, first:last].rearrange("p t (c i) -> p c t i", i=4),
+            )
+
+        group(nc.scalar.copy, 0, 0, HALF)
+        group(nc.vector.tensor_copy, 1, HALF - B_VECTOR, HALF)
+        group(nc.scalar.copy, 1, 0, HALF - B_VECTOR)
+        for h in range(2):
+            nc.vector.quantize_mx(
+                out=ds_codes[h][:].bitcast(FP8X4),
+                scales=ds_scales[h][:],
+                in_=ds_grouped[h][:].rearrange("p n t -> p (n t)"),
+            )
+
+        dk_sb = [keep.tile([P, N], F32, name=f"dk_sb{b}") for b in range(2)]
+        for b in range(2):
+            d_cols = slice(b * P, (b + 1) * P)
+            for h in range(2):
+                cols = slice(h * HALF, (h + 1) * HALF)
+                dk = psum.tile([P, HALF], F32, name="bank0" if b == h == 0 else "bank1")
+                nc.tensor.matmul_mx(
+                    out=dk[:],
+                    lhsT=q_codes[:, d_cols].bitcast(FP8X4),
+                    lhsT_scale=q_scales[:, d_cols],
+                    rhs=ds_codes[h][:].bitcast(FP8X4),
+                    rhs_scale=ds_scales[h][:],
+                    start=True,
+                    stop=True,
+                )
+                nc.scalar.copy(dk_sb[b][:, cols], dk[:])
+                if b == 0:
+                    nc.vector.tensor_copy(
+                        windows[b][:].indirect(offsets[:, h * 16 : (h + 1) * 16]), dk_sb[b][:, cols]
+                    )
+            if b == 1:
+                nc.vector.tensor_copy(windows[b][:].indirect(offsets[:]), dk_sb[b][:])
+            nc.sync.dma_start(out[b * P : (b + 1) * P, :], windows[b][:])

@@ -12,13 +12,13 @@ U16 = mybir.dt.uint16
 U8 = mybir.dt.uint8
 FP8X4 = mybir.dt.float8_e4m3fn_x4
 MULT = mybir.AluOpType.mult
-SUB = mybir.AluOpType.subtract
+ADD = mybir.AluOpType.add
 
 P = 128
 J = 4
 HALF = N // 2
-M_VECTOR = 88
-B_VECTOR = 144
+M_VECTOR = 24
+B_VECTOR = 160
 
 
 def tile_attend_bwd_kernel(tc, doT, vT, p, delta, qm, offs, out):
@@ -26,6 +26,23 @@ def tile_attend_bwd_kernel(tc, doT, vT, p, delta, qm, offs, out):
     with ExitStack() as ctx:
         keep = ctx.enter_context(tc.tile_pool(name="keep", bufs=1))
         psum = ctx.enter_context(tc.psum_pool(name="psum", bufs=1))
+
+        def quantize(name, grouped, words):
+            codes = keep.tile([P, words], U32, name=f"{name}_codes", align_bytes=64)
+            scales = keep.tile([P, words], U8, name=f"{name}_scales", align_bytes=64)
+            nc.vector.quantize_mx(out=codes[:].bitcast(FP8X4), scales=scales[:], in_=grouped)
+            return codes, scales
+
+        def product(bank, lhs, lhs_cols, rhs):
+            nc.tensor.matmul_mx(
+                out=bank,
+                lhsT=lhs[0][:, lhs_cols].bitcast(FP8X4),
+                lhsT_scale=lhs[1][:, lhs_cols],
+                rhs=rhs[0][:].bitcast(FP8X4),
+                rhs_scale=rhs[1][:],
+                start=True,
+                stop=True,
+            )
 
         offsets = keep.tile([P, N // 16], U16, name="offsets")
         v_view = vT.rearrange("(p t) n -> p t n", t=J)
@@ -36,19 +53,19 @@ def tile_attend_bwd_kernel(tc, doT, vT, p, delta, qm, offs, out):
             v_planes.append(plane)
             if t == 0:
                 nc.sync.dma_start(offsets[:], offs)
+                delta_sb = keep.tile([P, J], F32, name="delta_sb")
+                nc.sync.dma_start(delta_sb[:], delta[0].rearrange("(p t) o -> p (t o)", t=J))
+                minus_delta = keep.tile([P, J], F32, name="minus_delta")
+                nc.scalar.mul(minus_delta[:], delta_sb[:], -1.0)
         do_raw = keep.tile([P, J, NQ], F32, name="do_raw")
         nc.sync.dma_start(do_raw[:], doT[0].rearrange("(p j) q -> p j q", j=J))
-        delta_sb = keep.tile([P, J], F32, name="delta_sb")
-        nc.sync.dma_start(delta_sb[:], delta[0].rearrange("(p t) o -> p (t o)", t=J))
         p_view = p[0].rearrange("(p t) n -> p t n", t=J)
-        p_halves = []
-        for h in range(2):
-            p_half = keep.tile([P, J, HALF], F32, name=f"p_half{h}")
-            nc.sync.dma_start(p_half[:], p_view[:, :, h * HALF : (h + 1) * HALF])
-            p_halves.append(p_half)
-            if h == 0:
-                q_raw = keep.tile([P, J, D], F32, name="q_raw")
-                nc.sync.dma_start(q_raw[:], qm[0].rearrange("(p t) d -> p t d", t=J))
+        p_halves = [keep.tile([P, J, HALF], F32, name=f"p_half{h}", align_bytes=64) for h in range(2)]
+        q_raw = keep.tile([P, J, D], F32, name="q_raw")
+        q_src = [q_raw[:, :, b * P : (b + 1) * P] for b in range(2)]
+        nc.sync.dma_start(p_halves[0][:], p_view[:, :, 0 * HALF : (0 + 1) * HALF])
+        nc.sync.dma_start(p_halves[1][:], p_view[:, :, 1 * HALF : (1 + 1) * HALF])
+        nc.sync.dma_start(q_raw[:], qm[0].rearrange("(p t) d -> p t d", t=J))
 
         windows = []
         for b in range(2):
@@ -64,99 +81,76 @@ def tile_attend_bwd_kernel(tc, doT, vT, p, delta, qm, offs, out):
                 v_grouped[:, h * HALF : (h + 1) * HALF, J - 1],
                 v_planes[J - 1][:].indirect(offsets[:, h * 16 : (h + 1) * 16]),
             )
-        v_codes = keep.tile([P, N], U32, name="v_codes", align_bytes=64)
-        v_scales = keep.tile([P, N], U8, name="v_scales", align_bytes=64)
-        for h in range(2):
-            cols = slice(h * HALF, (h + 1) * HALF)
-            nc.vector.quantize_mx(
-                out=v_codes[:, cols].bitcast(FP8X4),
-                scales=v_scales[:, cols],
-                in_=v_grouped[:, cols, :].rearrange("p n t -> p (n t)"),
-            )
+        v_mx = [
+            quantize(f"v{h}", v_grouped[:, h * HALF : (h + 1) * HALF, :].rearrange("p n t -> p (n t)"), HALF)
+            for h in range(2)
+        ]
 
         do_grouped = keep.tile([P, J, P, J], BF16, name="do_grouped", align_bytes=64)
         do_dst = do_grouped[:].rearrange("p t m j -> p m j t")
         do_src = do_raw[:].rearrange("p j (m t) -> p m j t", t=J)
-        nc.vector.tensor_copy(do_dst[:, :M_VECTOR], do_src[:, :M_VECTOR])
-        nc.scalar.copy(do_dst[:, M_VECTOR:], do_src[:, M_VECTOR:])
+        nc.vector.tensor_copy(do_dst[:, :, :, :2], do_src[:, :, :, :2])
+        nc.vector.tensor_copy(do_dst[:, :M_VECTOR, :, 2:], do_src[:, :M_VECTOR, :, 2:])
+        nc.scalar.copy(do_dst[:, M_VECTOR:, :, 2:], do_src[:, M_VECTOR:, :, 2:])
         do_flat = do_grouped[:].rearrange("p t m j -> p (t m j)")
-        do_codes = keep.tile([P, NQ], U32, name="do_codes", align_bytes=64)
-        do_scales = keep.tile([P, NQ], U8, name="do_scales", align_bytes=64)
-        for h in range(2):
-            w = slice(h * 256, (h + 1) * 256)
-            nc.vector.quantize_mx(
-                out=do_codes[:, w].bitcast(FP8X4), scales=do_scales[:, w], in_=do_flat[:, h * 1024 : (h + 1) * 1024]
-            )
+        do_mx = [quantize(f"do{u}", do_flat[:, u * 1024 : (u + 1) * 1024], 2 * P) for u in range(2)]
 
-        q_grouped = keep.tile([P, D, J], BF16, name="q_grouped", align_bytes=64)
-        nc.scalar.copy(
-            q_grouped[:].rearrange("p (c i) t -> p c t i", i=4), q_raw[:].rearrange("p t (c i) -> p c t i", i=4)
-        )
-        q_codes = keep.tile([P, D], U32, name="q_codes", align_bytes=64)
-        q_scales = keep.tile([P, D], U8, name="q_scales", align_bytes=64)
+        def interleave(copy, dst, src):
+            copy(dst.rearrange("p (c i) t -> p c t i", i=4), src.rearrange("p t (c i) -> p c t i", i=4))
 
-        nc.vector.quantize_mx(
-            out=q_codes[:].bitcast(FP8X4), scales=q_scales[:], in_=q_grouped[:].rearrange("p d t -> p (d t)")
-        )
+        def pool_copy(dst, src):
+            nc.gpsimd.tensor_scalar(dst, src.rearrange("p t n -> p n t"), 1.0, 0.0, MULT, ADD)
 
-        part = [keep.tile([P, J, HALF], F32, name=f"part{h}") for h in range(2)]
+        def flat(grouped):
+            return grouped[:].rearrange("p n t -> p (n t)")
+
+        part = [keep.tile([P, J, HALF], F32, name=f"part{h}", align_bytes=64) for h in range(2)]
         ds_grouped = [keep.tile([P, HALF, J], BF16, name=f"ds_grouped{h}", align_bytes=64) for h in range(2)]
-        ds_codes = [keep.tile([P, HALF], U32, name=f"ds_codes{h}", align_bytes=64) for h in range(2)]
-        ds_scales = [keep.tile([P, HALF], U8, name=f"ds_scales{h}", align_bytes=64) for h in range(2)]
-        for h in range(2):
-            cols = slice(h * HALF, (h + 1) * HALF)
-            for t in range(J):
-                dp = psum.tile([P, HALF], F32, name=f"bank{4 * h + t}")
-                q_cols = slice(t * P, (t + 1) * P)
-                nc.tensor.matmul_mx(
-                    out=dp[:],
-                    lhsT=do_codes[:, q_cols].bitcast(FP8X4),
-                    lhsT_scale=do_scales[:, q_cols],
-                    rhs=v_codes[:, cols].bitcast(FP8X4),
-                    rhs_scale=v_scales[:, cols],
-                    start=True,
-                    stop=True,
-                )
-                nc.vector.scalar_tensor_tensor(
-                    part[h][:, t, :], dp[:], delta_sb[:, t : t + 1], p_halves[h][:, t, :], SUB, MULT
-                )
+
+        def weigh(h, t):
+            dp = psum.tile([P, HALF], F32, name=f"bank{t}")
+            product(dp[:], do_mx[t // 2], slice((t % 2) * P, (t % 2 + 1) * P), v_mx[h])
+            nc.vector.scalar_tensor_tensor(
+                part[h][:, t, :], dp[:], minus_delta[:, t : t + 1], p_halves[h][:, t, :], ADD, MULT
+            )
 
         def group(copy, h, first, last):
-            copy(
-                ds_grouped[h][:, first:last].rearrange("p (c i) t -> p c t i", i=4),
-                part[h][:, :, first:last].rearrange("p t (c i) -> p c t i", i=4),
-            )
+            interleave(copy, ds_grouped[h][:, first:last], part[h][:, :, first:last])
 
-        group(nc.scalar.copy, 0, 0, HALF)
+        def scatter(b, first, last, values):
+            nc.vector.tensor_copy(windows[b][:].indirect(offsets[:, first // 16 : last // 16]), values)
+
+        def store(b):
+            nc.sync.dma_start(out[b * P : (b + 1) * P, :], windows[b][:])
+
+        every = slice(0, P)
+        for h in range(2):
+            for t in range(J):
+                weigh(h, t)
+            if h == 0:
+                group(nc.scalar.copy, 0, 0, HALF)
+        q_grouped0 = keep.tile([P, P, J], BF16, name="p_half1", align_bytes=64)
+        interleave(nc.vector.tensor_copy, q_grouped0[:], q_src[0])
+        ds_mx0 = quantize("ds0", flat(ds_grouped[0]), HALF)
+        q_mx0 = quantize("q0", flat(q_grouped0), P)
+        q_grouped1 = keep.tile([P, P, J], BF16, name="part0", align_bytes=64)
+        interleave(nc.scalar.copy, q_grouped1[:], q_src[1])
         group(nc.vector.tensor_copy, 1, HALF - B_VECTOR, HALF)
         group(nc.scalar.copy, 1, 0, HALF - B_VECTOR)
-        for h in range(2):
-            nc.vector.quantize_mx(
-                out=ds_codes[h][:].bitcast(FP8X4),
-                scales=ds_scales[h][:],
-                in_=ds_grouped[h][:].rearrange("p n t -> p (n t)"),
-            )
+        q_mx1 = quantize("q1", flat(q_grouped1), P)
+        ds_mx1 = quantize("ds1", flat(ds_grouped[1]), HALF)
+        ds_mx = [ds_mx0, ds_mx1]
+        q_mx = [q_mx0, q_mx1]
 
         dk_sb = [keep.tile([P, N], F32, name=f"dk_sb{b}") for b in range(2)]
         for b in range(2):
-            d_cols = slice(b * P, (b + 1) * P)
             for h in range(2):
                 cols = slice(h * HALF, (h + 1) * HALF)
-                dk = psum.tile([P, HALF], F32, name="bank0" if b == h == 0 else "bank1")
-                nc.tensor.matmul_mx(
-                    out=dk[:],
-                    lhsT=q_codes[:, d_cols].bitcast(FP8X4),
-                    lhsT_scale=q_scales[:, d_cols],
-                    rhs=ds_codes[h][:].bitcast(FP8X4),
-                    rhs_scale=ds_scales[h][:],
-                    start=True,
-                    stop=True,
-                )
+                dk = psum.tile([P, HALF], F32, name="bank4" if b == h == 0 else "bank5")
+                product(dk[:], q_mx[b], every, ds_mx[h])
                 nc.scalar.copy(dk_sb[b][:, cols], dk[:])
                 if b == 0:
-                    nc.vector.tensor_copy(
-                        windows[b][:].indirect(offsets[:, h * 16 : (h + 1) * 16]), dk_sb[b][:, cols]
-                    )
+                    scatter(b, h * HALF, (h + 1) * HALF, dk_sb[b][:, cols])
             if b == 1:
-                nc.vector.tensor_copy(windows[b][:].indirect(offsets[:]), dk_sb[b][:])
-            nc.sync.dma_start(out[b * P : (b + 1) * P, :], windows[b][:])
+                scatter(b, 0, N, dk_sb[b][:])
+            store(b)

@@ -17,8 +17,9 @@ ADD = mybir.AluOpType.add
 P = 128
 J = 4
 HALF = N // 2
-M_VECTOR = 24
-B_VECTOR = 160
+M_VECTOR = (88, 56)
+PIECE = 192
+A_VECTOR = 96
 
 
 def tile_attend_bwd_kernel(tc, doT, vT, p, delta, qm, offs, out):
@@ -61,16 +62,19 @@ def tile_attend_bwd_kernel(tc, doT, vT, p, delta, qm, offs, out):
         nc.sync.dma_start(do_raw[:], doT[0].rearrange("(p j) q -> p j q", j=J))
         p_view = p[0].rearrange("(p t) n -> p t n", t=J)
         p_halves = [keep.tile([P, J, HALF], F32, name=f"p_half{h}", align_bytes=64) for h in range(2)]
-        q_raw = keep.tile([P, J, D], F32, name="q_raw")
-        q_src = [q_raw[:, :, b * P : (b + 1) * P] for b in range(2)]
+        q_view = qm[0].rearrange("(p t) d -> p t d", t=J)
+        q_raw = [keep.tile([P, J, P], F32, name=f"q_raw{b}") for b in range(2)]
         nc.sync.dma_start(p_halves[0][:], p_view[:, :, 0 * HALF : (0 + 1) * HALF])
+        nc.sync.dma_start(q_raw[0][:], q_view[:, :, 0 * P : (0 + 1) * P])
         nc.sync.dma_start(p_halves[1][:], p_view[:, :, 1 * HALF : (1 + 1) * HALF])
-        nc.sync.dma_start(q_raw[:], qm[0].rearrange("(p t) d -> p t d", t=J))
+        nc.sync.dma_start(q_raw[1][:], q_view[:, :, 1 * P : (1 + 1) * P])
+
+        q_src = [q_raw[b][:] for b in range(2)]
 
         windows = []
         for b in range(2):
             window = keep.tile([P, T], F32, name=f"window{b}")
-            (nc.vector if b == 0 else nc.gpsimd).memset(window[:], 0.0)
+            nc.vector.memset(window[:], 0.0)
             windows.append(window)
 
         v_grouped = keep.tile([P, N, J], BF16, name="v_grouped", align_bytes=64)
@@ -89,17 +93,17 @@ def tile_attend_bwd_kernel(tc, doT, vT, p, delta, qm, offs, out):
         do_grouped = keep.tile([P, J, P, J], BF16, name="do_grouped", align_bytes=64)
         do_dst = do_grouped[:].rearrange("p t m j -> p m j t")
         do_src = do_raw[:].rearrange("p j (m t) -> p m j t", t=J)
-        nc.vector.tensor_copy(do_dst[:, :, :, :2], do_src[:, :, :, :2])
-        nc.vector.tensor_copy(do_dst[:, :M_VECTOR, :, 2:], do_src[:, :M_VECTOR, :, 2:])
-        nc.scalar.copy(do_dst[:, M_VECTOR:, :, 2:], do_src[:, M_VECTOR:, :, 2:])
+        for u, m_vector in enumerate(M_VECTOR):
+            pair = slice(2 * u, 2 * u + 2)
+            nc.vector.tensor_copy(do_dst[:, :m_vector, :, pair], do_src[:, :m_vector, :, pair])
+            nc.scalar.copy(do_dst[:, m_vector:, :, pair], do_src[:, m_vector:, :, pair])
         do_flat = do_grouped[:].rearrange("p t m j -> p (t m j)")
-        do_mx = [quantize(f"do{u}", do_flat[:, u * 1024 : (u + 1) * 1024], 2 * P) for u in range(2)]
+        do_first = [quantize(f"do{t}", do_flat[:, t * 512 : (t + 1) * 512], P) for t in range(2)]
+        do_rest = quantize("do_rest", do_flat[:, 1024:], 2 * P)
+        do_mx = [(do_first[0], slice(0, P)), (do_first[1], slice(0, P)), (do_rest, slice(0, P)), (do_rest, slice(P, 2 * P))]
 
         def interleave(copy, dst, src):
             copy(dst.rearrange("p (c i) t -> p c t i", i=4), src.rearrange("p t (c i) -> p c t i", i=4))
-
-        def pool_copy(dst, src):
-            nc.gpsimd.tensor_scalar(dst, src.rearrange("p t n -> p n t"), 1.0, 0.0, MULT, ADD)
 
         def flat(grouped):
             return grouped[:].rearrange("p n t -> p (n t)")
@@ -109,7 +113,7 @@ def tile_attend_bwd_kernel(tc, doT, vT, p, delta, qm, offs, out):
 
         def weigh(h, t):
             dp = psum.tile([P, HALF], F32, name=f"bank{t}")
-            product(dp[:], do_mx[t // 2], slice((t % 2) * P, (t % 2 + 1) * P), v_mx[h])
+            product(dp[:], do_mx[t][0], do_mx[t][1], v_mx[h])
             nc.vector.scalar_tensor_tensor(
                 part[h][:, t, :], dp[:], minus_delta[:, t : t + 1], p_halves[h][:, t, :], ADD, MULT
             )
@@ -124,33 +128,39 @@ def tile_attend_bwd_kernel(tc, doT, vT, p, delta, qm, offs, out):
             nc.sync.dma_start(out[b * P : (b + 1) * P, :], windows[b][:])
 
         every = slice(0, P)
-        for h in range(2):
-            for t in range(J):
-                weigh(h, t)
-            if h == 0:
-                group(nc.scalar.copy, 0, 0, HALF)
-        q_grouped0 = keep.tile([P, P, J], BF16, name="p_half1", align_bytes=64)
-        interleave(nc.vector.tensor_copy, q_grouped0[:], q_src[0])
-        ds_mx0 = quantize("ds0", flat(ds_grouped[0]), HALF)
+        zeros = keep.tile([P, PIECE], F32, name="zeros")
+        nc.vector.memset(zeros[:], 0.0)
+        q_grouped0 = keep.tile([P, P, J], BF16, name="q_grouped0", align_bytes=64)
+        interleave(nc.scalar.copy, q_grouped0[:], q_src[0])
         q_mx0 = quantize("q0", flat(q_grouped0), P)
+        for t in range(J):
+            weigh(0, t)
+        group(nc.vector.tensor_copy, 0, HALF - A_VECTOR, HALF)
+        group(nc.scalar.copy, 0, 0, HALF - A_VECTOR)
+        ds_mx0 = quantize("ds0", flat(ds_grouped[0]), HALF)
+        for t in range(J):
+            weigh(1, t)
+        dk_sb = [keep.tile([P, N], F32, name=f"dk_sb{b}") for b in range(2)]
+
+        def key_gradient(copy, b, h, q_mx, ds_mx):
+            dk = psum.tile([P, HALF], F32, name=f"bank{4 + 2 * b + h}")
+            product(dk[:], q_mx, every, ds_mx)
+            copy(dk_sb[b][:, h * HALF : (h + 1) * HALF], dk[:])
+
+        key_gradient(nc.scalar.copy, 0, 0, q_mx0, ds_mx0)
         q_grouped1 = keep.tile([P, P, J], BF16, name="part0", align_bytes=64)
         interleave(nc.scalar.copy, q_grouped1[:], q_src[1])
-        group(nc.vector.tensor_copy, 1, HALF - B_VECTOR, HALF)
-        group(nc.scalar.copy, 1, 0, HALF - B_VECTOR)
         q_mx1 = quantize("q1", flat(q_grouped1), P)
+        group(nc.scalar.copy, 1, 0, HALF)
+        scatter(0, 0, HALF, dk_sb[0][:, :HALF])
         ds_mx1 = quantize("ds1", flat(ds_grouped[1]), HALF)
-        ds_mx = [ds_mx0, ds_mx1]
-        q_mx = [q_mx0, q_mx1]
-
-        dk_sb = [keep.tile([P, N], F32, name=f"dk_sb{b}") for b in range(2)]
-        for b in range(2):
-            for h in range(2):
-                cols = slice(h * HALF, (h + 1) * HALF)
-                dk = psum.tile([P, HALF], F32, name="bank4" if b == h == 0 else "bank5")
-                product(dk[:], q_mx[b], every, ds_mx[h])
-                nc.scalar.copy(dk_sb[b][:, cols], dk[:])
-                if b == 0:
-                    scatter(b, h * HALF, (h + 1) * HALF, dk_sb[b][:, cols])
-            if b == 1:
-                scatter(b, 0, N, dk_sb[b][:])
-            store(b)
+        key_gradient(nc.scalar.copy, 1, 0, q_mx1, ds_mx0)
+        nc.vector.tensor_tensor(
+            windows[1][:].indirect(offsets[:, : PIECE // 16]), dk_sb[1][:, :PIECE], zeros[:], ADD
+        )
+        key_gradient(nc.scalar.copy, 0, 1, q_mx0, ds_mx1)
+        scatter(0, HALF, N, dk_sb[0][:, HALF:])
+        store(0)
+        key_gradient(nc.scalar.copy, 1, 1, q_mx1, ds_mx1)
+        scatter(1, PIECE, N, dk_sb[1][:, PIECE:])
+        store(1)

@@ -17,7 +17,6 @@ ADD = mybir.AluOpType.add
 P = 128
 J = 4
 HALF = N // 2
-M_VECTOR = (88, 56)
 PIECE = 192
 A_VECTOR = 96
 
@@ -58,18 +57,20 @@ def tile_attend_bwd_kernel(tc, doT, vT, p, delta, qm, offs, out):
                 nc.sync.dma_start(delta_sb[:], delta[0].rearrange("(p t) o -> p (t o)", t=J))
                 minus_delta = keep.tile([P, J], F32, name="minus_delta")
                 nc.scalar.mul(minus_delta[:], delta_sb[:], -1.0)
-        do_raw = keep.tile([P, J, NQ], F32, name="do_raw")
-        nc.sync.dma_start(do_raw[:], doT[0].rearrange("(p j) q -> p j q", j=J))
+        do_view = doT[0].rearrange("(p j) q -> p j q", j=J)
+        do_raw = []
+        for u in range(2):
+            do_half = keep.tile([P, J, NQ // 2], F32, name=f"do_half{u}")
+            nc.sync.dma_start(do_half[:], do_view[:, :, u * (NQ // 2) : (u + 1) * (NQ // 2)])
+            do_raw.append(do_half)
         p_view = p[0].rearrange("(p t) n -> p t n", t=J)
         p_halves = [keep.tile([P, J, HALF], F32, name=f"p_half{h}", align_bytes=64) for h in range(2)]
-        q_view = qm[0].rearrange("(p t) d -> p t d", t=J)
-        q_raw = [keep.tile([P, J, P], F32, name=f"q_raw{b}") for b in range(2)]
+        q_raw = keep.tile([P, J, D], F32, name="q_raw")
         nc.sync.dma_start(p_halves[0][:], p_view[:, :, 0 * HALF : (0 + 1) * HALF])
-        nc.sync.dma_start(q_raw[0][:], q_view[:, :, 0 * P : (0 + 1) * P])
+        nc.sync.dma_start(q_raw[:], qm[0].rearrange("(p t) d -> p t d", t=J))
         nc.sync.dma_start(p_halves[1][:], p_view[:, :, 1 * HALF : (1 + 1) * HALF])
-        nc.sync.dma_start(q_raw[1][:], q_view[:, :, 1 * P : (1 + 1) * P])
 
-        q_src = [q_raw[b][:] for b in range(2)]
+        q_src = [q_raw[:, :, b * P : (b + 1) * P] for b in range(2)]
 
         windows = []
         for b in range(2):
@@ -90,16 +91,15 @@ def tile_attend_bwd_kernel(tc, doT, vT, p, delta, qm, offs, out):
             for h in range(2)
         ]
 
-        do_grouped = keep.tile([P, J, P, J], BF16, name="do_grouped", align_bytes=64)
-        do_dst = do_grouped[:].rearrange("p t m j -> p m j t")
-        do_src = do_raw[:].rearrange("p j (m t) -> p m j t", t=J)
-        for u, m_vector in enumerate(M_VECTOR):
-            pair = slice(2 * u, 2 * u + 2)
-            nc.vector.tensor_copy(do_dst[:, :m_vector, :, pair], do_src[:, :m_vector, :, pair])
-            nc.scalar.copy(do_dst[:, m_vector:, :, pair], do_src[:, m_vector:, :, pair])
-        do_flat = do_grouped[:].rearrange("p t m j -> p (t m j)")
-        do_first = [quantize(f"do{t}", do_flat[:, t * 512 : (t + 1) * 512], P) for t in range(2)]
-        do_rest = quantize("do_rest", do_flat[:, 1024:], 2 * P)
+        do_src = [half[:].rearrange("p j (m t) -> p m j t", t=J) for half in do_raw]
+        do_grouped = [keep.tile([P, 2, P, J], BF16, name=f"do_grouped{u}", align_bytes=64) for u in range(2)]
+        do_dst = [pair[:].rearrange("p t m j -> p m j t") for pair in do_grouped]
+        for u in range(2):
+            nc.scalar.copy(do_dst[u][:, : P // 2], do_src[0][:, :, :, 2 * u : 2 * u + 2])
+        nc.vector.tensor_copy(do_dst[0][:, P // 2 :], do_src[1][:, :, :, :2])
+        nc.scalar.copy(do_dst[1][:, P // 2 :], do_src[1][:, :, :, 2:])
+        do_first = [quantize(f"do{t}", do_grouped[0][:, t].rearrange("p m j -> p (m j)"), P) for t in range(2)]
+        do_rest = quantize("do_rest", do_grouped[1][:].rearrange("p t m j -> p (t m j)"), 2 * P)
         do_mx = [(do_first[0], slice(0, P)), (do_first[1], slice(0, P)), (do_rest, slice(0, P)), (do_rest, slice(P, 2 * P))]
 
         def interleave(copy, dst, src):

@@ -18,7 +18,7 @@ P = 128
 J = 4
 HALF = N // 2
 PIECE = 192
-A_VECTOR = 96
+A_VECTOR = 144
 
 
 def tile_attend_bwd_kernel(tc, doT, vT, p, delta, qm, offs, out):

@@ -18,6 +18,7 @@ P = 128
 J = 4
 HALF = N // 2
 PIECE = 192
+M_VECTOR = 24
 A_VECTOR = 144
 
 
@@ -65,12 +66,14 @@ def tile_attend_bwd_kernel(tc, doT, vT, p, delta, qm, offs, out):
             do_raw.append(do_half)
         p_view = p[0].rearrange("(p t) n -> p t n", t=J)
         p_halves = [keep.tile([P, J, HALF], F32, name=f"p_half{h}", align_bytes=64) for h in range(2)]
-        q_raw = keep.tile([P, J, D], F32, name="q_raw")
+        q_view = qm[0].rearrange("(p t) d -> p t d", t=J)
+        q_raw = [keep.tile([P, J, P], F32, name=f"q_raw{b}") for b in range(2)]
         nc.sync.dma_start(p_halves[0][:], p_view[:, :, 0 * HALF : (0 + 1) * HALF])
-        nc.sync.dma_start(q_raw[:], qm[0].rearrange("(p t) d -> p t d", t=J))
+        nc.sync.dma_start(q_raw[0][:], q_view[:, :, 0 * P : (0 + 1) * P])
         nc.sync.dma_start(p_halves[1][:], p_view[:, :, 1 * HALF : (1 + 1) * HALF])
+        nc.sync.dma_start(q_raw[1][:], q_view[:, :, 1 * P : (1 + 1) * P])
 
-        q_src = [q_raw[:, :, b * P : (b + 1) * P] for b in range(2)]
+        q_src = [q_raw[b][:] for b in range(2)]
 
         windows = []
         for b in range(2):
@@ -97,7 +100,8 @@ def tile_attend_bwd_kernel(tc, doT, vT, p, delta, qm, offs, out):
         for u in range(2):
             nc.scalar.copy(do_dst[u][:, : P // 2], do_src[0][:, :, :, 2 * u : 2 * u + 2])
         nc.vector.tensor_copy(do_dst[0][:, P // 2 :], do_src[1][:, :, :, :2])
-        nc.scalar.copy(do_dst[1][:, P // 2 :], do_src[1][:, :, :, 2:])
+        nc.vector.tensor_copy(do_dst[1][:, P - M_VECTOR :], do_src[1][:, P // 2 - M_VECTOR :, :, 2:])
+        nc.scalar.copy(do_dst[1][:, P // 2 : P - M_VECTOR], do_src[1][:, : P // 2 - M_VECTOR, :, 2:])
         do_first = [quantize(f"do{t}", do_grouped[0][:, t].rearrange("p m j -> p (m j)"), P) for t in range(2)]
         do_rest = quantize("do_rest", do_grouped[1][:].rearrange("p t m j -> p (t m j)"), 2 * P)
         do_mx = [(do_first[0], slice(0, P)), (do_first[1], slice(0, P)), (do_rest, slice(0, P)), (do_rest, slice(P, 2 * P))]

@@ -17,9 +17,9 @@ ADD = mybir.AluOpType.add
 P = 128
 J = 4
 HALF = N // 2
-PIECE = 192
+PIECE = 64
 M_VECTOR = 24
-A_VECTOR = 144
+QUARTER = N // 4
 
 
 def tile_attend_bwd_kernel(tc, doT, vT, p, delta, qm, offs, out):
@@ -34,13 +34,13 @@ def tile_attend_bwd_kernel(tc, doT, vT, p, delta, qm, offs, out):
             nc.vector.quantize_mx(out=codes[:].bitcast(FP8X4), scales=scales[:], in_=grouped)
             return codes, scales
 
-        def product(bank, lhs, lhs_cols, rhs):
+        def product(bank, lhs, lhs_cols, rhs, rhs_cols=slice(0, HALF)):
             nc.tensor.matmul_mx(
                 out=bank,
                 lhsT=lhs[0][:, lhs_cols].bitcast(FP8X4),
                 lhsT_scale=lhs[1][:, lhs_cols],
-                rhs=rhs[0][:].bitcast(FP8X4),
-                rhs_scale=rhs[1][:],
+                rhs=rhs[0][:, rhs_cols].bitcast(FP8X4),
+                rhs_scale=rhs[1][:, rhs_cols],
                 start=True,
                 stop=True,
             )
@@ -65,13 +65,15 @@ def tile_attend_bwd_kernel(tc, doT, vT, p, delta, qm, offs, out):
             nc.sync.dma_start(do_half[:], do_view[:, :, u * (NQ // 2) : (u + 1) * (NQ // 2)])
             do_raw.append(do_half)
         p_view = p[0].rearrange("(p t) n -> p t n", t=J)
-        p_halves = [keep.tile([P, J, HALF], F32, name=f"p_half{h}", align_bytes=64) for h in range(2)]
         q_view = qm[0].rearrange("(p t) d -> p t d", t=J)
         q_raw = [keep.tile([P, J, P], F32, name=f"q_raw{b}") for b in range(2)]
-        nc.sync.dma_start(p_halves[0][:], p_view[:, :, 0 * HALF : (0 + 1) * HALF])
-        nc.sync.dma_start(q_raw[0][:], q_view[:, :, 0 * P : (0 + 1) * P])
-        nc.sync.dma_start(p_halves[1][:], p_view[:, :, 1 * HALF : (1 + 1) * HALF])
-        nc.sync.dma_start(q_raw[1][:], q_view[:, :, 1 * P : (1 + 1) * P])
+        p_quarters = [keep.tile([P, J, QUARTER], F32, name=f"p_quarter{c}", align_bytes=64) for c in range(2)]
+        p_pairs = [keep.tile([P, 2, HALF], F32, name=f"p_pair{u}", align_bytes=64) for u in range(2)]
+        for c in range(2):
+            nc.sync.dma_start(q_raw[c][:], q_view[:, :, c * P : (c + 1) * P])
+            nc.sync.dma_start(p_quarters[c][:], p_view[:, :, c * QUARTER : (c + 1) * QUARTER])
+        for u in range(2):
+            nc.sync.dma_start(p_pairs[u][:], p_view[:, 2 * u : 2 * u + 2, HALF:])
 
         q_src = [q_raw[b][:] for b in range(2)]
 
@@ -112,18 +114,17 @@ def tile_attend_bwd_kernel(tc, doT, vT, p, delta, qm, offs, out):
         def flat(grouped):
             return grouped[:].rearrange("p n t -> p (n t)")
 
-        part = [keep.tile([P, J, HALF], F32, name=f"part{h}", align_bytes=64) for h in range(2)]
+        part_quarters = [keep.tile([P, J, QUARTER], F32, name=f"part_quarter{c}", align_bytes=64) for c in range(2)]
+        part_half = keep.tile([P, J, HALF], F32, name="part_half", align_bytes=64)
         ds_grouped = [keep.tile([P, HALF, J], BF16, name=f"ds_grouped{h}", align_bytes=64) for h in range(2)]
 
-        def weigh(h, t):
-            dp = psum.tile([P, HALF], F32, name=f"bank{t}")
+        def weight_gradient(h, t):
+            dp = psum.tile([P, HALF], F32, name=f"bank{t + 2}")
             product(dp[:], do_mx[t][0], do_mx[t][1], v_mx[h])
-            nc.vector.scalar_tensor_tensor(
-                part[h][:, t, :], dp[:], minus_delta[:, t : t + 1], p_halves[h][:, t, :], ADD, MULT
-            )
+            return dp
 
-        def group(copy, h, first, last):
-            interleave(copy, ds_grouped[h][:, first:last], part[h][:, :, first:last])
+        def weigh(dst, dp, t, weights, shift=minus_delta):
+            nc.vector.scalar_tensor_tensor(dst, dp, shift[:, t : t + 1], weights, ADD, MULT)
 
         def scatter(b, first, last, values):
             nc.vector.tensor_copy(windows[b][:].indirect(offsets[:, first // 16 : last // 16]), values)
@@ -131,40 +132,53 @@ def tile_attend_bwd_kernel(tc, doT, vT, p, delta, qm, offs, out):
         def store(b):
             nc.sync.dma_start(out[b * P : (b + 1) * P, :], windows[b][:])
 
+        def scatter_sum(b, first, last, values):
+            nc.vector.tensor_tensor(
+                windows[b][:].indirect(offsets[:, first // 16 : last // 16]), values, zeros[:, : last - first], ADD
+            )
+
         every = slice(0, P)
-        zeros = keep.tile([P, PIECE], F32, name="zeros")
+        zeros = keep.tile([P, QUARTER], F32, name="zeros")
         nc.vector.memset(zeros[:], 0.0)
-        q_grouped0 = keep.tile([P, P, J], BF16, name="q_grouped0", align_bytes=64)
-        interleave(nc.scalar.copy, q_grouped0[:], q_src[0])
-        q_mx0 = quantize("q0", flat(q_grouped0), P)
+        q_mx = []
+        for b in range(2):
+            q_grouped = keep.tile([P, P, J], BF16, name=f"q_grouped{b}", align_bytes=64)
+            interleave(nc.scalar.copy, q_grouped[:], q_src[b])
+            q_mx.append(quantize(f"q{b}", flat(q_grouped), P))
+        for c in range(2):
+            for t in ((0, 1, 2, 3), (2, 3, 0, 1))[c]:
+                dp = psum.tile([P, QUARTER], F32, name=f"bank{t + 2 * c * (t // 2)}")
+                product(dp[:], do_mx[t][0], do_mx[t][1], v_mx[0], slice(c * QUARTER, (c + 1) * QUARTER))
+                weigh(part_quarters[c][:, t, :], dp[:], t, p_quarters[c][:, t, :])
+        ds_quarters = []
+        for c in range(2):
+            grouped = ds_grouped[0][:, c * QUARTER : (c + 1) * QUARTER]
+            interleave(nc.scalar.copy, grouped, part_quarters[c][:])
+            ds_quarters.append(quantize(f"ds_quarter{c}", grouped.rearrange("p n t -> p (n t)"), QUARTER))
         for t in range(J):
-            weigh(0, t)
-        group(nc.vector.tensor_copy, 0, HALF - A_VECTOR, HALF)
-        group(nc.scalar.copy, 0, 0, HALF - A_VECTOR)
-        ds_mx0 = quantize("ds0", flat(ds_grouped[0]), HALF)
-        for t in range(J):
-            weigh(1, t)
-        dk_sb = [keep.tile([P, N], F32, name=f"dk_sb{b}") for b in range(2)]
-
-        def key_gradient(copy, b, h, q_mx, ds_mx):
-            dk = psum.tile([P, HALF], F32, name=f"bank{4 + 2 * b + h}")
-            product(dk[:], q_mx, every, ds_mx)
-            copy(dk_sb[b][:, h * HALF : (h + 1) * HALF], dk[:])
-
-        key_gradient(nc.scalar.copy, 0, 0, q_mx0, ds_mx0)
-        q_grouped1 = keep.tile([P, P, J], BF16, name="part0", align_bytes=64)
-        interleave(nc.scalar.copy, q_grouped1[:], q_src[1])
-        q_mx1 = quantize("q1", flat(q_grouped1), P)
-        group(nc.scalar.copy, 1, 0, HALF)
-        scatter(0, 0, HALF, dk_sb[0][:, :HALF])
+            weigh(part_half[:, t, :], weight_gradient(1, t)[:], t, p_pairs[t // 2][:, t % 2, :])
+        whole_quarter = slice(0, QUARTER)
+        for b in range(2):
+            dk = psum.tile([P, QUARTER], F32, name=f"bank{6 + b}")
+            product(dk[:], q_mx[b], every, ds_quarters[0], whole_quarter)
+            dk_first = keep.tile([P, QUARTER], F32, name=f"dk_first{b}")
+            nc.scalar.copy(dk_first[:], dk[:])
+            scatter_sum(b, 0, QUARTER, dk_first[:])
+        interleave(nc.scalar.copy, ds_grouped[1][:], part_half[:])
         ds_mx1 = quantize("ds1", flat(ds_grouped[1]), HALF)
-        key_gradient(nc.scalar.copy, 1, 0, q_mx1, ds_mx0)
-        nc.vector.tensor_tensor(
-            windows[1][:].indirect(offsets[:, : PIECE // 16]), dk_sb[1][:, :PIECE], zeros[:], ADD
-        )
-        key_gradient(nc.scalar.copy, 0, 1, q_mx0, ds_mx1)
-        scatter(0, HALF, N, dk_sb[0][:, HALF:])
+        dk = psum.tile([P, 2, QUARTER], F32, name="bank0")
+        for b in range(2):
+            product(dk[:, b, :], q_mx[b], every, ds_quarters[1], whole_quarter)
+        dk_late = keep.tile([P, N], F32, name="part_half", align_bytes=64)
+        nc.scalar.copy(dk_late[:, :HALF], dk[:].rearrange("p b n -> p (b n)"))
+        scatter_sum(0, QUARTER, HALF, dk_late[:, :QUARTER])
+        scatter_sum(1, QUARTER, QUARTER + PIECE, dk_late[:, QUARTER : QUARTER + PIECE])
+        dk_last = keep.tile([P, HALF], F32, name="dk_last")
+        for b, dst in ((0, dk_last[:]), (1, dk_late[:, HALF:])):
+            dk = psum.tile([P, HALF], F32, name=f"bank{1 + b}")
+            product(dk[:], q_mx[b], every, ds_mx1)
+            nc.scalar.copy(dst, dk[:])
+        scatter(0, HALF, N, dk_last[:])
         store(0)
-        key_gradient(nc.scalar.copy, 1, 1, q_mx1, ds_mx1)
-        scatter(1, PIECE, N, dk_sb[1][:, PIECE:])
+        scatter(1, QUARTER + PIECE, N, dk_late[:, QUARTER + PIECE :])
         store(1)

@@ -17,7 +17,8 @@ ADD = mybir.AluOpType.add
 P = 128
 J = 4
 HALF = N // 2
-PIECE = 64
+FIRST = 96
+SECOND = 160
 M_VECTOR = 24
 QUARTER = N // 4
 
@@ -158,27 +159,25 @@ def tile_attend_bwd_kernel(tc, doT, vT, p, delta, qm, offs, out):
         for t in range(J):
             weigh(part_half[:, t, :], weight_gradient(1, t)[:], t, p_pairs[t // 2][:, t % 2, :])
         whole_quarter = slice(0, QUARTER)
-        for b in range(2):
+        dk_sb = keep.tile([P, 2, N], F32, name="dk_sb")
+        for b, last in ((0, QUARTER), (1, FIRST)):
             dk = psum.tile([P, QUARTER], F32, name=f"bank{6 + b}")
             product(dk[:], q_mx[b], every, ds_quarters[0], whole_quarter)
-            dk_first = keep.tile([P, QUARTER], F32, name=f"dk_first{b}")
-            nc.scalar.copy(dk_first[:], dk[:])
-            scatter_sum(b, 0, QUARTER, dk_first[:])
+            nc.scalar.copy(dk_sb[:, b, :QUARTER], dk[:])
+            scatter_sum(b, 0, last, dk_sb[:, b, :last])
         interleave(nc.scalar.copy, ds_grouped[1][:], part_half[:])
         ds_mx1 = quantize("ds1", flat(ds_grouped[1]), HALF)
         dk = psum.tile([P, 2, QUARTER], F32, name="bank0")
         for b in range(2):
             product(dk[:, b, :], q_mx[b], every, ds_quarters[1], whole_quarter)
-        dk_late = keep.tile([P, N], F32, name="part_half", align_bytes=64)
-        nc.scalar.copy(dk_late[:, :HALF], dk[:].rearrange("p b n -> p (b n)"))
-        scatter_sum(0, QUARTER, HALF, dk_late[:, :QUARTER])
-        scatter_sum(1, QUARTER, QUARTER + PIECE, dk_late[:, QUARTER : QUARTER + PIECE])
-        dk_last = keep.tile([P, HALF], F32, name="dk_last")
-        for b, dst in ((0, dk_last[:]), (1, dk_late[:, HALF:])):
+        nc.scalar.copy(dk_sb[:, :, QUARTER:HALF], dk[:])
+        scatter_sum(0, QUARTER, HALF, dk_sb[:, 0, QUARTER:HALF])
+        scatter_sum(1, FIRST, SECOND, dk_sb[:, 1, FIRST:SECOND])
+        for b in range(2):
             dk = psum.tile([P, HALF], F32, name=f"bank{1 + b}")
             product(dk[:], q_mx[b], every, ds_mx1)
-            nc.scalar.copy(dst, dk[:])
-        scatter(0, HALF, N, dk_last[:])
+            nc.scalar.copy(dk_sb[:, b, HALF:], dk[:])
+        scatter(0, HALF, N, dk_sb[:, 0, HALF:])
         store(0)
-        scatter(1, QUARTER + PIECE, N, dk_late[:, QUARTER + PIECE :])
+        scatter(1, SECOND, N, dk_sb[:, 1, SECOND:])
         store(1)

@@ -173,10 +173,13 @@ def tile_attend_bwd_kernel(tc, doT, vT, p, delta, qm, offs, out):
         nc.scalar.copy(dk_sb[:, :, QUARTER:HALF], dk[:])
         scatter_sum(0, QUARTER, HALF, dk_sb[:, 0, QUARTER:HALF])
         scatter_sum(1, FIRST, SECOND, dk_sb[:, 1, FIRST:SECOND])
-        for b in range(2):
-            dk = psum.tile([P, HALF], F32, name=f"bank{1 + b}")
-            product(dk[:], q_mx[b], every, ds_mx1)
-            nc.scalar.copy(dk_sb[:, b, HALF:], dk[:])
+        for c in range(2):
+            dk = psum.tile([P, QUARTER], F32, name=f"bank{1 + c}")
+            product(dk[:], q_mx[0], every, ds_mx1, slice(c * QUARTER, (c + 1) * QUARTER))
+            nc.scalar.copy(dk_sb[:, 0, HALF + c * QUARTER : HALF + (c + 1) * QUARTER], dk[:])
+        dk = psum.tile([P, HALF], F32, name="bank3")
+        product(dk[:], q_mx[1], every, ds_mx1)
+        nc.scalar.copy(dk_sb[:, 1, HALF:], dk[:])
         scatter(0, HALF, N, dk_sb[:, 0, HALF:])
         store(0)
         scatter(1, SECOND, N, dk_sb[:, 1, SECOND:])

@@ -19,7 +19,7 @@ J = 4
 HALF = N // 2
 FIRST = 96
 SECOND = 160
-M_VECTOR = 24
+M_VECTOR = 32
 QUARTER = N // 4
 
 
@@ -60,11 +60,8 @@ def tile_attend_bwd_kernel(tc, doT, vT, p, delta, qm, offs, out):
                 minus_delta = keep.tile([P, J], F32, name="minus_delta")
                 nc.scalar.mul(minus_delta[:], delta_sb[:], -1.0)
         do_view = doT[0].rearrange("(p j) q -> p j q", j=J)
-        do_raw = []
-        for u in range(2):
-            do_half = keep.tile([P, J, NQ // 2], F32, name=f"do_half{u}")
-            nc.sync.dma_start(do_half[:], do_view[:, :, u * (NQ // 2) : (u + 1) * (NQ // 2)])
-            do_raw.append(do_half)
+        do_raw = keep.tile([P, J, NQ], F32, name="do_raw")
+        nc.sync.dma_start(do_raw[:], do_view)
         p_view = p[0].rearrange("(p t) n -> p t n", t=J)
         q_view = qm[0].rearrange("(p t) d -> p t d", t=J)
         q_raw = [keep.tile([P, J, P], F32, name=f"q_raw{b}") for b in range(2)]
@@ -97,14 +94,12 @@ def tile_attend_bwd_kernel(tc, doT, vT, p, delta, qm, offs, out):
             for h in range(2)
         ]
 
-        do_src = [half[:].rearrange("p j (m t) -> p m j t", t=J) for half in do_raw]
+        do_src = do_raw[:].rearrange("p j (m t) -> p m j t", t=J)
         do_grouped = [keep.tile([P, 2, P, J], BF16, name=f"do_grouped{u}", align_bytes=64) for u in range(2)]
         do_dst = [pair[:].rearrange("p t m j -> p m j t") for pair in do_grouped]
-        for u in range(2):
-            nc.scalar.copy(do_dst[u][:, : P // 2], do_src[0][:, :, :, 2 * u : 2 * u + 2])
-        nc.vector.tensor_copy(do_dst[0][:, P // 2 :], do_src[1][:, :, :, :2])
-        nc.vector.tensor_copy(do_dst[1][:, P - M_VECTOR :], do_src[1][:, P // 2 - M_VECTOR :, :, 2:])
-        nc.scalar.copy(do_dst[1][:, P // 2 : P - M_VECTOR], do_src[1][:, : P // 2 - M_VECTOR, :, 2:])
+        nc.vector.tensor_copy(do_dst[0], do_src[:, :, :, :2])
+        nc.vector.tensor_copy(do_dst[1][:, P - M_VECTOR :], do_src[:, P - M_VECTOR :, :, 2:])
+        nc.scalar.copy(do_dst[1][:, : P - M_VECTOR], do_src[:, : P - M_VECTOR, :, 2:])
         do_first = [quantize(f"do{t}", do_grouped[0][:, t].rearrange("p m j -> p (m j)"), P) for t in range(2)]
         do_rest = quantize("do_rest", do_grouped[1][:].rearrange("p t m j -> p (t m j)"), 2 * P)
         do_mx = [(do_first[0], slice(0, P)), (do_first[1], slice(0, P)), (do_rest, slice(0, P)), (do_rest, slice(P, 2 * P))]

@@ -19,7 +19,7 @@ J = 4
 HALF = N // 2
 FIRST = 96
 SECOND = 160
-M_VECTOR = 32
+M_VECTOR = 24
 QUARTER = N // 4
 
 
@@ -60,8 +60,9 @@ def tile_attend_bwd_kernel(tc, doT, vT, p, delta, qm, offs, out):
                 minus_delta = keep.tile([P, J], F32, name="minus_delta")
                 nc.scalar.mul(minus_delta[:], delta_sb[:], -1.0)
         do_view = doT[0].rearrange("(p j) q -> p j q", j=J)
-        do_raw = keep.tile([P, J, NQ], F32, name="do_raw")
-        nc.sync.dma_start(do_raw[:], do_view)
+        do_raw = [keep.tile([P, J, NQ // 2], F32, name=f"do_raw{h}") for h in range(2)]
+        for h in range(2):
+            nc.sync.dma_start(do_raw[h][:], do_view[:, :, h * (NQ // 2) : (h + 1) * (NQ // 2)])
         p_view = p[0].rearrange("(p t) n -> p t n", t=J)
         q_view = qm[0].rearrange("(p t) d -> p t d", t=J)
         q_raw = [keep.tile([P, J, P], F32, name=f"q_raw{b}") for b in range(2)]
@@ -94,12 +95,15 @@ def tile_attend_bwd_kernel(tc, doT, vT, p, delta, qm, offs, out):
             for h in range(2)
         ]
 
-        do_src = do_raw[:].rearrange("p j (m t) -> p m j t", t=J)
+        do_src = [half[:].rearrange("p j (m t) -> p m j t", t=J) for half in do_raw]
         do_grouped = [keep.tile([P, 2, P, J], BF16, name=f"do_grouped{u}", align_bytes=64) for u in range(2)]
         do_dst = [pair[:].rearrange("p t m j -> p m j t") for pair in do_grouped]
-        nc.vector.tensor_copy(do_dst[0], do_src[:, :, :, :2])
-        nc.vector.tensor_copy(do_dst[1][:, P - M_VECTOR :], do_src[:, P - M_VECTOR :, :, 2:])
-        nc.scalar.copy(do_dst[1][:, : P - M_VECTOR], do_src[:, : P - M_VECTOR, :, 2:])
+        M = P // 2
+        for u in range(2):
+            nc.scalar.copy(do_dst[u][:, :M], do_src[0][:, :, :, 2 * u : 2 * u + 2])
+        nc.vector.tensor_copy(do_dst[0][:, M:], do_src[1][:, :, :, :2])
+        nc.vector.tensor_copy(do_dst[1][:, P - M_VECTOR :], do_src[1][:, M - M_VECTOR :, :, 2:])
+        nc.scalar.copy(do_dst[1][:, M : P - M_VECTOR], do_src[1][:, : M - M_VECTOR, :, 2:])
         do_first = [quantize(f"do{t}", do_grouped[0][:, t].rearrange("p m j -> p (m j)"), P) for t in range(2)]
         do_rest = quantize("do_rest", do_grouped[1][:].rearrange("p t m j -> p (t m j)"), 2 * P)
         do_mx = [(do_first[0], slice(0, P)), (do_first[1], slice(0, P)), (do_rest, slice(0, P)), (do_rest, slice(P, 2 * P))]
@@ -136,23 +140,24 @@ def tile_attend_bwd_kernel(tc, doT, vT, p, delta, qm, offs, out):
         every = slice(0, P)
         zeros = keep.tile([P, QUARTER], F32, name="zeros")
         nc.vector.memset(zeros[:], 0.0)
-        q_mx = []
+        q_grouped = [keep.tile([P, P, J], BF16, name=f"q_grouped{b}", align_bytes=64) for b in range(2)]
         for b in range(2):
-            q_grouped = keep.tile([P, P, J], BF16, name=f"q_grouped{b}", align_bytes=64)
-            interleave(nc.scalar.copy, q_grouped[:], q_src[b])
-            q_mx.append(quantize(f"q{b}", flat(q_grouped), P))
+            interleave(nc.scalar.copy, q_grouped[b][:], q_src[b])
+        q_mx = [quantize("q0", flat(q_grouped[0]), P)]
         for c in range(2):
             for t in ((0, 1, 2, 3), (2, 3, 0, 1))[c]:
                 dp = psum.tile([P, QUARTER], F32, name=f"bank{t + 2 * c * (t // 2)}")
                 product(dp[:], do_mx[t][0], do_mx[t][1], v_mx[0], slice(c * QUARTER, (c + 1) * QUARTER))
                 weigh(part_quarters[c][:, t, :], dp[:], t, p_quarters[c][:, t, :])
-        ds_quarters = []
+        q_mx.append(quantize("q1", flat(q_grouped[1]), P))
+        grouped = [ds_grouped[0][:, c * QUARTER : (c + 1) * QUARTER] for c in range(2)]
         for c in range(2):
-            grouped = ds_grouped[0][:, c * QUARTER : (c + 1) * QUARTER]
-            interleave(nc.scalar.copy, grouped, part_quarters[c][:])
-            ds_quarters.append(quantize(f"ds_quarter{c}", grouped.rearrange("p n t -> p (n t)"), QUARTER))
+            interleave(nc.scalar.copy, grouped[c], part_quarters[c][:])
         for t in range(J):
             weigh(part_half[:, t, :], weight_gradient(1, t)[:], t, p_pairs[t // 2][:, t % 2, :])
+            if t == 0:
+                ds_quarters = [quantize("ds_quarter0", grouped[0].rearrange("p n t -> p (n t)"), QUARTER)]
+        ds_quarters.append(quantize("ds_quarter1", grouped[1].rearrange("p n t -> p (n t)"), QUARTER))
         whole_quarter = slice(0, QUARTER)
         dk_sb = keep.tile([P, 2, N], F32, name="dk_sb")
         for b, last in ((0, QUARTER), (1, FIRST)):

@@ -13,6 +13,7 @@ U8 = mybir.dt.uint8
 FP8X4 = mybir.dt.float8_e4m3fn_x4
 MULT = mybir.AluOpType.mult
 ADD = mybir.AluOpType.add
+SUBTRACT = mybir.AluOpType.subtract
 
 P = 128
 J = 4
@@ -55,14 +56,12 @@ def tile_attend_bwd_kernel(tc, doT, vT, p, delta, qm, offs, out):
             v_planes.append(plane)
             if t == 0:
                 nc.sync.dma_start(offsets[:], offs)
-                delta_sb = keep.tile([P, J], F32, name="delta_sb")
-                nc.sync.dma_start(delta_sb[:], delta[0].rearrange("(p t) o -> p (t o)", t=J))
-                minus_delta = keep.tile([P, J], F32, name="minus_delta")
-                nc.scalar.mul(minus_delta[:], delta_sb[:], -1.0)
         do_view = doT[0].rearrange("(p j) q -> p j q", j=J)
         do_raw = [keep.tile([P, J, NQ // 2], F32, name=f"do_raw{h}") for h in range(2)]
         for h in range(2):
             nc.sync.dma_start(do_raw[h][:], do_view[:, :, h * (NQ // 2) : (h + 1) * (NQ // 2)])
+        delta_sb = keep.tile([P, J], F32, name="delta_sb")
+        nc.sync.dma_start(delta_sb[:], delta[0].rearrange("(p t) o -> p (t o)", t=J))
         p_view = p[0].rearrange("(p t) n -> p t n", t=J)
         q_view = qm[0].rearrange("(p t) d -> p t d", t=J)
         q_raw = [keep.tile([P, J, P], F32, name=f"q_raw{b}") for b in range(2)]
@@ -123,8 +122,8 @@ def tile_attend_bwd_kernel(tc, doT, vT, p, delta, qm, offs, out):
             product(dp[:], do_mx[t][0], do_mx[t][1], v_mx[h])
             return dp
 
-        def weigh(dst, dp, t, weights, shift=minus_delta):
-            nc.vector.scalar_tensor_tensor(dst, dp, shift[:, t : t + 1], weights, ADD, MULT)
+        def weigh(dst, dp, t, weights, shift=delta_sb):
+            nc.vector.scalar_tensor_tensor(dst, dp, shift[:, t : t + 1], weights, SUBTRACT, MULT)
 
         def scatter(b, first, last, values):
             nc.vector.tensor_copy(windows[b][:].indirect(offsets[:, first // 16 : last // 16]), values)
@@ -139,7 +138,7 @@ def tile_attend_bwd_kernel(tc, doT, vT, p, delta, qm, offs, out):
 
         every = slice(0, P)
         zeros = keep.tile([P, QUARTER], F32, name="zeros")
-        nc.vector.memset(zeros[:], 0.0)
+        nc.scalar.copy(zeros[:], windows[0][:, :QUARTER])
         q_grouped = [keep.tile([P, P, J], BF16, name=f"q_grouped{b}", align_bytes=64) for b in range(2)]
         for b in range(2):
             interleave(nc.scalar.copy, q_grouped[b][:], q_src[b])

@@ -51,22 +51,22 @@ def tile_attend_bwd_kernel(tc, doT, vT, p, delta, qm, offs, out):
         v_view = vT.rearrange("(p t) n -> p t n", t=J)
         v_planes = []
         for t in range(J):
-            plane = keep.tile([P, T], F32, name=f"plane{t}")
+            plane = keep.tile([P, T], F32, name=f"plane{t}", align_bytes=256)
             nc.sync.dma_start(plane[:], v_view[:, t, :])
             v_planes.append(plane)
             if t == 0:
                 nc.sync.dma_start(offsets[:], offs)
         do_view = doT[0].rearrange("(p j) q -> p j q", j=J)
-        do_raw = [keep.tile([P, J, NQ // 2], F32, name=f"do_raw{h}") for h in range(2)]
+        do_raw = [keep.tile([P, J, NQ // 2], F32, name=f"do_raw{h}", align_bytes=256) for h in range(2)]
         for h in range(2):
             nc.sync.dma_start(do_raw[h][:], do_view[:, :, h * (NQ // 2) : (h + 1) * (NQ // 2)])
         delta_sb = keep.tile([P, J], F32, name="delta_sb")
         nc.sync.dma_start(delta_sb[:], delta[0].rearrange("(p t) o -> p (t o)", t=J))
         p_view = p[0].rearrange("(p t) n -> p t n", t=J)
         q_view = qm[0].rearrange("(p t) d -> p t d", t=J)
-        q_raw = [keep.tile([P, J, P], F32, name=f"q_raw{b}") for b in range(2)]
-        p_quarters = [keep.tile([P, J, QUARTER], F32, name=f"p_quarter{c}", align_bytes=64) for c in range(2)]
-        p_pairs = [keep.tile([P, 2, HALF], F32, name=f"p_pair{u}", align_bytes=64) for u in range(2)]
+        q_raw = [keep.tile([P, J, P], F32, name=f"q_raw{b}", align_bytes=256) for b in range(2)]
+        p_quarters = [keep.tile([P, J, QUARTER], F32, name=f"p_quarter{c}", align_bytes=256) for c in range(2)]
+        p_pairs = [keep.tile([P, 2, HALF], F32, name=f"p_pair{u}", align_bytes=256) for u in range(2)]
         for c in range(2):
             nc.sync.dma_start(q_raw[c][:], q_view[:, :, c * P : (c + 1) * P])
             nc.sync.dma_start(p_quarters[c][:], p_view[:, :, c * QUARTER : (c + 1) * QUARTER])
@@ -77,7 +77,7 @@ def tile_attend_bwd_kernel(tc, doT, vT, p, delta, qm, offs, out):
 
         windows = []
         for b in range(2):
-            window = keep.tile([P, T], F32, name=f"window{b}")
+            window = keep.tile([P, T], F32, name=f"window{b}", align_bytes=256)
             nc.vector.memset(window[:], 0.0)
             windows.append(window)
 

@@ -20,7 +20,6 @@ J = 4
 HALF = N // 2
 FIRST = 96
 SECOND = 160
-M_VECTOR = 24
 QUARTER = N // 4
 
 
@@ -30,8 +29,8 @@ def tile_attend_bwd_kernel(tc, doT, vT, p, delta, qm, offs, out):
         keep = ctx.enter_context(tc.tile_pool(name="keep", bufs=1))
         psum = ctx.enter_context(tc.psum_pool(name="psum", bufs=1))
 
-        def quantize(name, grouped, words):
-            codes = keep.tile([P, words], U32, name=f"{name}_codes", align_bytes=64)
+        def quantize(name, grouped, words, tag=None):
+            codes = keep.tile([P, words], U32, name=f"{name}_codes", tag=tag or f"{name}_codes", align_bytes=256)
             scales = keep.tile([P, words], U8, name=f"{name}_scales", align_bytes=64)
             nc.vector.quantize_mx(out=codes[:].bitcast(FP8X4), scales=scales[:], in_=grouped)
             return codes, scales
@@ -89,10 +88,7 @@ def tile_attend_bwd_kernel(tc, doT, vT, p, delta, qm, offs, out):
                 v_grouped[:, h * HALF : (h + 1) * HALF, J - 1],
                 v_planes[J - 1][:].indirect(offsets[:, h * 16 : (h + 1) * 16]),
             )
-        v_mx = [
-            quantize(f"v{h}", v_grouped[:, h * HALF : (h + 1) * HALF, :].rearrange("p n t -> p (n t)"), HALF)
-            for h in range(2)
-        ]
+        v_mx = [quantize("v0", v_grouped[:, :HALF, :].rearrange("p n t -> p (n t)"), HALF)]
 
         do_src = [half[:].rearrange("p j (m t) -> p m j t", t=J) for half in do_raw]
         do_grouped = [keep.tile([P, 2, P, J], BF16, name=f"do_grouped{u}", align_bytes=64) for u in range(2)]
@@ -101,8 +97,8 @@ def tile_attend_bwd_kernel(tc, doT, vT, p, delta, qm, offs, out):
         for u in range(2):
             nc.scalar.copy(do_dst[u][:, :M], do_src[0][:, :, :, 2 * u : 2 * u + 2])
         nc.vector.tensor_copy(do_dst[0][:, M:], do_src[1][:, :, :, :2])
-        nc.vector.tensor_copy(do_dst[1][:, P - M_VECTOR :], do_src[1][:, M - M_VECTOR :, :, 2:])
-        nc.scalar.copy(do_dst[1][:, M : P - M_VECTOR], do_src[1][:, : M - M_VECTOR, :, 2:])
+        nc.scalar.copy(do_dst[1][:, M:], do_src[1][:, :, :, 2:])
+        v_mx.append(quantize("v1", v_grouped[:, HALF:, :].rearrange("p n t -> p (n t)"), HALF, tag="do_raw0"))
         do_first = [quantize(f"do{t}", do_grouped[0][:, t].rearrange("p m j -> p (m j)"), P) for t in range(2)]
         do_rest = quantize("do_rest", do_grouped[1][:].rearrange("p t m j -> p (t m j)"), 2 * P)
         do_mx = [(do_first[0], slice(0, P)), (do_first[1], slice(0, P)), (do_rest, slice(0, P)), (do_rest, slice(P, 2 * P))]

from contextlib import ExitStack

import concourse.mybir as mybir

NQ, N, T, D, DV = 512, 512, 2048, 256, 512
FLOPS = 2 * NQ * N * DV + 2 * D * N * NQ

F32 = mybir.dt.float32
BF16 = mybir.dt.bfloat16
U32 = mybir.dt.uint32
U16 = mybir.dt.uint16
U8 = mybir.dt.uint8
FP8X4 = mybir.dt.float8_e4m3fn_x4
MULT = mybir.AluOpType.mult
ADD = mybir.AluOpType.add
SUBTRACT = mybir.AluOpType.subtract

P = 128
J = 4
HALF = N // 2
FIRST = 96
SECOND = 160
QUARTER = N // 4


def tile_attend_bwd_kernel(tc, doT, vT, p, delta, qm, offs, out):
    nc = tc.nc
    with ExitStack() as ctx:
        keep = ctx.enter_context(tc.tile_pool(name="keep", bufs=1))
        psum = ctx.enter_context(tc.psum_pool(name="psum", bufs=1))

        def quantize(name, grouped, words, tag=None):
            codes = keep.tile([P, words], U32, name=f"{name}_codes", tag=tag or f"{name}_codes", align_bytes=256)
            scales = keep.tile([P, words], U8, name=f"{name}_scales", align_bytes=64)
            nc.vector.quantize_mx(out=codes[:].bitcast(FP8X4), scales=scales[:], in_=grouped)
            return codes, scales

        def product(bank, lhs, lhs_cols, rhs, rhs_cols=slice(0, HALF)):
            nc.tensor.matmul_mx(
                out=bank,
                lhsT=lhs[0][:, lhs_cols].bitcast(FP8X4),
                lhsT_scale=lhs[1][:, lhs_cols],
                rhs=rhs[0][:, rhs_cols].bitcast(FP8X4),
                rhs_scale=rhs[1][:, rhs_cols],
                start=True,
                stop=True,
            )

        offsets = keep.tile([P, N // 16], U16, name="offsets")
        v_view = vT.rearrange("(p t) n -> p t n", t=J)
        v_planes = []
        for t in range(J):
            plane = keep.tile([P, T], F32, name=f"plane{t}", align_bytes=256)
            nc.sync.dma_start(plane[:], v_view[:, t, :])
            v_planes.append(plane)
            if t == 0:
                nc.sync.dma_start(offsets[:], offs)
        do_view = doT[0].rearrange("(p j) q -> p j q", j=J)
        do_raw = [keep.tile([P, J, NQ // 2], F32, name=f"do_raw{h}", align_bytes=256) for h in range(2)]
        for h in range(2):
            nc.sync.dma_start(do_raw[h][:], do_view[:, :, h * (NQ // 2) : (h + 1) * (NQ // 2)])
        delta_sb = keep.tile([P, J], F32, name="delta_sb")
        nc.sync.dma_start(delta_sb[:], delta[0].rearrange("(p t) o -> p (t o)", t=J))
        p_view = p[0].rearrange("(p t) n -> p t n", t=J)
        q_view = qm[0].rearrange("(p t) d -> p t d", t=J)
        q_raw = [keep.tile([P, J, P], F32, name=f"q_raw{b}", align_bytes=256) for b in range(2)]
        p_quarters = [keep.tile([P, J, QUARTER], F32, name=f"p_quarter{c}", align_bytes=256) for c in range(2)]
        p_pairs = [keep.tile([P, 2, HALF], F32, name=f"p_pair{u}", align_bytes=256) for u in range(2)]
        for c in range(2):
            nc.sync.dma_start(q_raw[c][:], q_view[:, :, c * P : (c + 1) * P])
            nc.sync.dma_start(p_quarters[c][:], p_view[:, :, c * QUARTER : (c + 1) * QUARTER])
        for u in range(2):
            nc.sync.dma_start(p_pairs[u][:], p_view[:, 2 * u : 2 * u + 2, HALF:])

        q_src = [q_raw[b][:] for b in range(2)]

        windows = []
        for b in range(2):
            window = keep.tile([P, T], F32, name=f"window{b}", align_bytes=256)
            nc.vector.memset(window[:], 0.0)
            windows.append(window)

        v_grouped = keep.tile([P, N, J], BF16, name="v_grouped", align_bytes=64)
        for t in range(J - 1):
            nc.vector.tensor_copy(v_grouped[:, :, t], v_planes[t][:].indirect(offsets[:]))
        for h in range(2):
            nc.vector.tensor_copy(
                v_grouped[:, h * HALF : (h + 1) * HALF, J - 1],
                v_planes[J - 1][:].indirect(offsets[:, h * 16 : (h + 1) * 16]),
            )
        v_mx = [quantize("v0", v_grouped[:, :HALF, :].rearrange("p n t -> p (n t)"), HALF)]

        do_src = [half[:].rearrange("p j (m t) -> p m j t", t=J) for half in do_raw]
        do_grouped = [keep.tile([P, 2, P, J], BF16, name=f"do_grouped{u}", align_bytes=64) for u in range(2)]
        do_dst = [pair[:].rearrange("p t m j -> p m j t") for pair in do_grouped]
        M = P // 2
        for u in range(2):
            nc.scalar.copy(do_dst[u][:, :M], do_src[0][:, :, :, 2 * u : 2 * u + 2])
        nc.vector.tensor_copy(do_dst[0][:, M:], do_src[1][:, :, :, :2])
        nc.scalar.copy(do_dst[1][:, M:], do_src[1][:, :, :, 2:])
        v_mx.append(quantize("v1", v_grouped[:, HALF:, :].rearrange("p n t -> p (n t)"), HALF, tag="do_raw0"))
        do_first = [quantize(f"do{t}", do_grouped[0][:, t].rearrange("p m j -> p (m j)"), P) for t in range(2)]
        do_rest = quantize("do_rest", do_grouped[1][:].rearrange("p t m j -> p (t m j)"), 2 * P)
        do_mx = [(do_first[0], slice(0, P)), (do_first[1], slice(0, P)), (do_rest, slice(0, P)), (do_rest, slice(P, 2 * P))]

        def interleave(copy, dst, src):
            copy(dst.rearrange("p (c i) t -> p c t i", i=4), src.rearrange("p t (c i) -> p c t i", i=4))

        def flat(grouped):
            return grouped[:].rearrange("p n t -> p (n t)")

        part_quarters = [keep.tile([P, J, QUARTER], F32, name=f"part_quarter{c}", align_bytes=64) for c in range(2)]
        part_half = keep.tile([P, J, HALF], F32, name="part_half", align_bytes=64)
        ds_grouped = [keep.tile([P, HALF, J], BF16, name=f"ds_grouped{h}", align_bytes=64) for h in range(2)]

        def weight_gradient(h, t):
            dp = psum.tile([P, HALF], F32, name=f"bank{t + 2}")
            product(dp[:], do_mx[t][0], do_mx[t][1], v_mx[h])
            return dp

        def weigh(dst, dp, t, weights, shift=delta_sb):
            nc.vector.scalar_tensor_tensor(dst, dp, shift[:, t : t + 1], weights, SUBTRACT, MULT)

        def scatter(b, first, last, values):
            nc.vector.tensor_copy(windows[b][:].indirect(offsets[:, first // 16 : last // 16]), values)

        def store(b):
            nc.sync.dma_start(out[b * P : (b + 1) * P, :], windows[b][:])

        def scatter_sum(b, first, last, values):
            nc.vector.tensor_tensor(
                windows[b][:].indirect(offsets[:, first // 16 : last // 16]), values, zeros[:, : last - first], ADD
            )

        every = slice(0, P)
        zeros = keep.tile([P, QUARTER], F32, name="zeros")
        nc.scalar.copy(zeros[:], windows[0][:, :QUARTER])
        q_grouped = [keep.tile([P, P, J], BF16, name=f"q_grouped{b}", align_bytes=64) for b in range(2)]
        for b in range(2):
            interleave(nc.scalar.copy, q_grouped[b][:], q_src[b])
        q_mx = [quantize("q0", flat(q_grouped[0]), P)]
        for c in range(2):
            for t in ((0, 1, 2, 3), (2, 3, 0, 1))[c]:
                dp = psum.tile([P, QUARTER], F32, name=f"bank{t + 2 * c * (t // 2)}")
                product(dp[:], do_mx[t][0], do_mx[t][1], v_mx[0], slice(c * QUARTER, (c + 1) * QUARTER))
                weigh(part_quarters[c][:, t, :], dp[:], t, p_quarters[c][:, t, :])
        q_mx.append(quantize("q1", flat(q_grouped[1]), P))
        grouped = [ds_grouped[0][:, c * QUARTER : (c + 1) * QUARTER] for c in range(2)]
        for c in range(2):
            interleave(nc.scalar.copy, grouped[c], part_quarters[c][:])
        for t in range(J):
            weigh(part_half[:, t, :], weight_gradient(1, t)[:], t, p_pairs[t // 2][:, t % 2, :])
            if t == 0:
                ds_quarters = [quantize("ds_quarter0", grouped[0].rearrange("p n t -> p (n t)"), QUARTER)]
        ds_quarters.append(quantize("ds_quarter1", grouped[1].rearrange("p n t -> p (n t)"), QUARTER))
        whole_quarter = slice(0, QUARTER)
        dk_sb = keep.tile([P, 2, N], F32, name="dk_sb")
        for b, last in ((0, QUARTER), (1, FIRST)):
            dk = psum.tile([P, QUARTER], F32, name=f"bank{6 + b}")
            product(dk[:], q_mx[b], every, ds_quarters[0], whole_quarter)
            nc.scalar.copy(dk_sb[:, b, :QUARTER], dk[:])
            scatter_sum(b, 0, last, dk_sb[:, b, :last])
        interleave(nc.scalar.copy, ds_grouped[1][:], part_half[:])
        ds_mx1 = quantize("ds1", flat(ds_grouped[1]), HALF)
        dk = psum.tile([P, 2, QUARTER], F32, name="bank0")
        for b in range(2):
            product(dk[:, b, :], q_mx[b], every, ds_quarters[1], whole_quarter)
        nc.scalar.copy(dk_sb[:, :, QUARTER:HALF], dk[:])
        scatter_sum(0, QUARTER, HALF, dk_sb[:, 0, QUARTER:HALF])
        scatter_sum(1, FIRST, SECOND, dk_sb[:, 1, FIRST:SECOND])
        for c in range(2):
            dk = psum.tile([P, QUARTER], F32, name=f"bank{1 + c}")
            product(dk[:], q_mx[0], every, ds_mx1, slice(c * QUARTER, (c + 1) * QUARTER))
            nc.scalar.copy(dk_sb[:, 0, HALF + c * QUARTER : HALF + (c + 1) * QUARTER], dk[:])
        dk = psum.tile([P, HALF], F32, name="bank3")
        product(dk[:], q_mx[1], every, ds_mx1)
        nc.scalar.copy(dk_sb[:, 1, HALF:], dk[:])
        scatter(0, HALF, N, dk_sb[:, 0, HALF:])
        store(0)
        scatter(1, SECOND, N, dk_sb[:, 1, SECOND:])
        store(1)
